import numpy as np
import ml_dtypes


def mxq(x, axis, fmt="e4m3"):
    dtype, down = {"e4m3": (ml_dtypes.float8_e4m3fn, 7), "e5m2": (ml_dtypes.float8_e5m2, 14)}[fmt]
    v = np.moveaxis(np.asarray(x, np.float32).astype(ml_dtypes.bfloat16).astype(np.float64), axis, -1)
    blocks = v.reshape(v.shape[:-1] + (-1, 32))
    amax = np.abs(blocks).max(-1, keepdims=True)
    byte = np.maximum(np.where(amax > 0, np.frexp(amax)[1] - 1 + 127, 0) - down, 1)
    scale = np.exp2(byte - 127.0)
    codes = (blocks / scale).astype(np.float32).astype(dtype).astype(np.float64)
    return np.moveaxis((codes * scale).reshape(v.shape), -1, axis)


WIDE = False


def mx_kscale(k):
    if not WIDE:
        return np.ones(k)
    levels = np.array([10, -10, 5, -5, 0])
    if k % 512:
        return np.exp2(np.random.permutation(np.resize(levels, k // 32))).repeat(32)
    a = np.empty((k // 512, 16))
    for p in range(k // 512):
        a[p, :8] = np.random.permutation(np.resize(levels, 8))
        for g in range(8):
            far = levels[np.abs(levels - a[p, g]) >= 10]
            a[p, g + 8] = far[np.random.randint(len(far))]
    return np.exp2(a.ravel()).repeat(32)


def f64(x):
    return np.asarray(x).astype(np.float64)


def striped(idx):
    return np.tile(np.asarray(idx).reshape(-1, 16).T, (8, 1)).astype(np.uint16)


def unstriped(offs):
    return offs[:16].T.reshape(-1).astype(np.int64)


E2M1 = np.array([0.0, 0.5, 1.0, 1.5, 2.0, 3.0, 4.0, 6.0, -0.0, -0.5, -1.0, -1.5, -2.0, -3.0, -4.0, -6.0])


def pack_weight(w, fmt):
    k, n = w.shape
    w = f64(np.asarray(w, np.float32).astype(ml_dtypes.bfloat16)).reshape(k // 32, 32, n)
    amax = np.abs(w).max(1)
    if fmt == "e4m3":
        byte = np.frexp(amax)[1] - 1 + 127 - 7
    else:
        mant, ex = np.frexp(amax / 6.0)
        byte = np.where(mant > 0.5, ex, ex - 1) + 127
    byte = np.clip(np.where(amax > 0, byte, 1), 1, 254)
    scaled = (w * np.exp2(127.0 - byte)[:, None, :]).reshape(k, n).astype(np.float32)
    by_word = np.ascontiguousarray(scaled.reshape(k // 512, 128, 4, n).transpose(0, 1, 3, 2))
    if fmt == "e4m3":
        words = by_word.astype(ml_dtypes.float8_e4m3fn).view(np.uint8)
    else:
        c = by_word.astype(ml_dtypes.float4_e2m1fn).view(np.uint8) & 0xF
        words = (c[..., 0::2] | (c[..., 1::2] << 4)).reshape(k // 512, 128, 2 * n)
    return np.ascontiguousarray(words), np.ascontiguousarray(byte.astype(np.uint8).reshape(k // 512, 16, n))


def unpack_weight(words, scales, fmt):
    g, _, n = scales.shape
    words = np.ascontiguousarray(words).reshape(g, 128, n, -1)
    if fmt == "e4m3":
        vals = words.view(ml_dtypes.float8_e4m3fn).astype(np.float64)
    else:
        nib = np.empty((g, 128, n, 4), np.uint8)
        nib[..., 0::2] = words & 0xF
        nib[..., 1::2] = words >> 4
        vals = E2M1[nib]
    vals = vals * np.repeat(np.exp2(scales.astype(np.float64) - 127.0), 8, axis=1)[..., None]
    return vals.transpose(0, 1, 3, 2).reshape(g * 512, n)


B, N, T, D, DV, NQ = 1, 1024, 4096, 512, 256, 128


def setup_inputs():
    n = np.random.standard_normal
    idx = np.random.permutation(T)[:B * N]
    s = mx_kscale(D)[:, None]
    u = np.ones(T)
    u[idx] = mx_kscale(B * N)
    r = np.random.uniform(0.5, 2.0, T)
    k = n((D, T)) / s
    v = n((DV, T)) / (u * r)
    kp = pack_weight(k, "e4m3")
    return {
        "qT": (n((B, D, NQ)) * s * (0.60 / np.sqrt(D))).astype(np.float32),
        "k_words": kp[0],
        "k_scales": kp[1],
        "vT": v.astype(np.float32),
        "vs": np.tile(u * r, (128, 1)).astype(np.float32),
        "kb": np.tile(n(T), (128, 1)).astype(np.float32),
        "offs": striped(idx),
    }


def reference(qT, k_words, k_scales, vT, vs, kb, offs):
    idx = unstriped(offs)
    k = unpack_weight(k_words, k_scales, "e4m3")
    v = f64(vT)
    pick = lambda x: x[:, idx].reshape(x.shape[0], B, N).transpose(1, 0, 2)
    q = f64(qT)
    score = mxq(q, 1, "e4m3").transpose(0, 2, 1) @ pick(k)
    score = score + pick(f64(kb))[:, :1, :]
    p = 1.0 / (1.0 + np.exp(-score))
    w = p * pick(f64(vs))[:, :1, :]
    y = mxq(w, 2, "e4m3") @ mxq(pick(v).transpose(0, 2, 1), 1, "e4m3")
    y = y / 16.0
    return y

@@ -1,0 +1,190 @@
+from contextlib import ExitStack
+
+import concourse.mybir as mybir
+from concourse.masks import make_identity
+
+F32 = mybir.dt.float32
+BF16 = mybir.dt.bfloat16
+I32 = mybir.dt.int32
+U32 = mybir.dt.uint32
+U16 = mybir.dt.uint16
+U8 = mybir.dt.uint8
+FP8X4 = mybir.dt.float8_e4m3fn_x4
+MULT = mybir.AluOpType.mult
+SIGMOID = mybir.ActivationFunctionType.Sigmoid
+
+P = 128
+TOKENS, SLOTS, D, DV, NQ = 4096, 1024, 512, 256, 128
+PACK = 4
+PASSES = SLOTS // (P * PACK)
+RUN = 8
+BLOCKS = SLOTS // (PACK * RUN)
+HALVES = DV // P
+KB_ROW = 4
+VS_ROW = 8
+
+FLOPS = 2 * NQ * SLOTS * (D + DV)
+BYTES = TOKENS * (D + D // 32 + 4 * DV + 8) + 4 * NQ * (D + DV) + 2 * SLOTS
+
+
+def dealt(ap):
+    return ap.rearrange("p (t b j) -> p b t j", t=PACK, j=RUN)
+
+
+def slot_tile(g, t):
+    start = (t * PASSES + g) * P
+    return slice(start, start + P)
+
+
+def tile_attend_sigmoid_topk_kernel(tc, qT, k_words, k_scales, vT, vs, kb, offs, out):
+    nc = tc.nc
+    with ExitStack() as ctx:
+        keep = ctx.enter_context(tc.tile_pool(name="keep", bufs=1))
+        psum = ctx.enter_context(tc.psum_pool(name="psum", bufs=1))
+        turn = ctx.enter_context(tc.psum_pool(name="turn", bufs=2))
+
+        offsets = keep.tile([P, SLOTS // 16], U16, name="offsets")
+        nc.sync.dma_start(offsets[:], offs)
+
+        q_raw = keep.tile([P, PACK, NQ], F32, name="q_raw")
+        nc.sync.dma_start(q_raw[:], qT[0].rearrange("(p t) q -> p t q", t=PACK))
+        word_pool = keep.tile([P, TOKENS], U32, name="word_pool")
+        nc.sync.dma_start(word_pool[:].bitcast(I32), k_words[0].rearrange("p n t -> p (n t)").bitcast(I32))
+
+        v_pool0 = keep.tile([P, TOKENS], F32, name="v_pool0")
+        nc.sync.dma_start(v_pool0[:], vT[0:P, :])
+
+        byte_pool = keep.tile([P, TOKENS], U8, name="byte_pool", tag="bytes_then_kb")
+        nc.vector.memset(byte_pool[:].bitcast(I32), 0)
+        for quad in range(4):
+            nc.scalar.dma_start(
+                byte_pool[32 * quad : 32 * quad + 4, :].bitcast(I32),
+                k_scales[0, 4 * quad : 4 * quad + 4, :].bitcast(I32),
+            )
+        kb_pool = keep.tile([P, TOKENS], F32, name="kb_pool", tag="kb_then_codes", align_bytes=64)
+        nc.vector.memset(kb_pool[:], 0.0)
+        nc.scalar.dma_start(kb_pool[KB_ROW : KB_ROW + 1, :], kb[0:1, :])
+        ident_f32 = keep.tile([P, P], F32, name="ident_f32")
+        make_identity(nc, ident_f32[:])
+        ident_bf16 = keep.tile([P, P], BF16, name="ident_bf16")
+        make_identity(nc, ident_bf16[:])
+
+        vs_pool = keep.tile([P, TOKENS], F32, name="vs_pool", tag="vs_then_values")
+        for start in range(0, TOKENS, 1024):
+            nc.gpsimd.memset(vs_pool[:, start : start + 1024], 0.0)
+        nc.sync.dma_start(vs_pool[VS_ROW : VS_ROW + 1, :], vs[0:1, :])
+
+        k_bytes_listed = keep.tile([P, SLOTS], U8, name="k_bytes_listed", tag="early1")
+        nc.vector.tensor_copy(k_bytes_listed[:], byte_pool[:].indirect(offsets[:]))
+        k_bytes = keep.tile([P, SLOTS], U8, name="k_bytes", align_bytes=64)
+        nc.vector.tensor_copy(
+            k_bytes[:].bitcast(I32).rearrange("p (t b w) -> p t b w", t=PACK, w=RUN // 4),
+            k_bytes_listed[:].bitcast(I32).rearrange("p (b t w) -> p t b w", t=PACK, w=RUN // 4),
+        )
+        kb_dealt = keep.tile([P, SLOTS], F32, name="kb_dealt", tag="bytes_then_kb")
+        nc.vector.tensor_copy(dealt(kb_dealt[:].bitcast(U32)), kb_pool[:].bitcast(U32).indirect(offsets[:]))
+        k_codes = keep.tile([P, SLOTS], U32, name="k_codes", tag="kb_then_codes", align_bytes=64)
+        nc.vector.tensor_copy(dealt(k_codes[:]), word_pool[:].indirect(offsets[:]))
+
+        q_packed = keep.tile([P, NQ, PACK], BF16, name="q_packed", align_bytes=64)
+        nc.scalar.copy(
+            q_packed[:].rearrange("p (c i) t -> p c t i", i=4),
+            q_raw[:].rearrange("p t (c i) -> p c t i", i=4),
+        )
+        q_codes = keep.tile([P, NQ], U32, name="q_codes", align_bytes=64)
+        q_bytes = keep.tile([P, NQ], U8, name="q_bytes", align_bytes=64)
+        nc.vector.quantize_mx(q_codes[:].bitcast(FP8X4), q_bytes[:], q_packed[:].rearrange("p q t -> p (q t)"))
+
+        v_pool1 = keep.tile([P, TOKENS], F32, name="v_pool1", tag="early1")
+        nc.sync.dma_start(v_pool1[:], vT[P : 2 * P, :])
+        v_pool = [v_pool0, v_pool1]
+
+        vs_dealt = keep.tile([P, SLOTS], F32, name="vs_dealt")
+        nc.vector.tensor_copy(dealt(vs_dealt[:].bitcast(U32)), vs_pool[:].bitcast(U32).indirect(offsets[:]))
+
+        probs = []
+        for g in range(PASSES):
+            kb_turned = turn.tile([P, PACK, P], F32, name="kb_turned", tag="turned")
+            for t in range(PACK):
+                nc.tensor.transpose(kb_turned[:, t, :], kb_dealt[:, slot_tile(g, t)], ident_f32[:])
+            kb_col = keep.tile([P, PACK], F32, name="kb_col%d" % g)
+            nc.scalar.copy(kb_col[:], kb_turned[:, :, KB_ROW])
+            scores = psum.tile([P, PACK, NQ], F32, name="scores%d" % g)
+            for t in range(PACK):
+                nc.tensor.matmul_mx(
+                    scores[:, t, :],
+                    lhsT=k_codes[:, slot_tile(g, t)].bitcast(FP8X4),
+                    lhsT_scale=k_bytes[:, slot_tile(g, t)],
+                    rhs=q_codes[:].bitcast(FP8X4),
+                    rhs_scale=q_bytes[:],
+                    start=True,
+                    stop=True,
+                )
+            prob = keep.tile([P, PACK, NQ], F32, name="prob%d" % g)
+            for t in range(PACK):
+                nc.scalar.activation(prob[:, t, :], scores[:, t, :], SIGMOID, bias=kb_col[:, t : t + 1])
+            probs.append(prob)
+
+        def gather_values(h, passes):
+            blocks = slice(passes[0] * BLOCKS // PASSES, (passes[-1] + 1) * BLOCKS // PASSES)
+            columns = slice(passes[0] * 32, (passes[-1] + 1) * 32)
+            nc.vector.tensor_copy(dealt(v_dealt[h][:])[:, blocks], v_pool[h][:].indirect(offsets[:, columns]))
+
+        def turn_values(h, g):
+            v_turned = turn.tile([P, PACK, P], BF16, name="v_turned", tag="turned")
+            for t in range(PACK):
+                nc.tensor.transpose(v_turned[:, t, :], v_dealt[h][:, slot_tile(g, t)], ident_bf16[:])
+            nc.scalar.copy(v_packed[h][g][:], v_turned[:].rearrange("p t e -> p e t"))
+
+        def quantise(packed, name):
+            codes = keep.tile([P, P], U32, name=name + "_codes", align_bytes=64)
+            scale_bytes = keep.tile([P, P], U8, name=name + "_bytes", align_bytes=64)
+            nc.vector.quantize_mx(codes[:].bitcast(FP8X4), scale_bytes[:], packed[:].rearrange("p c t -> p (c t)"))
+            return codes, scale_bytes
+
+        v_dealt = [
+            keep.tile([P, SLOTS], BF16, name="v_dealt0", tag="vs_then_values"),
+            keep.tile([P, SLOTS], BF16, name="v_dealt1"),
+        ]
+        v_packed = [
+            [keep.tile([P, P, PACK], BF16, name="v_packed%d%d" % (h, g), align_bytes=64) for g in range(PASSES)]
+            for h in range(HALVES)
+        ]
+
+        gather_values(0, [0, 1])
+        w_mx = []
+        for g in range(PASSES):
+            vs_turned = psum.tile([P, PACK, P], F32, name="vs_turned%d" % g)
+            for t in range(PACK):
+                nc.tensor.transpose(vs_turned[:, t, :], vs_dealt[:, slot_tile(g, t)], ident_f32[:])
+            w_packed = keep.tile([P, NQ, PACK], BF16, name="w_packed%d" % g, align_bytes=64)
+            nc.vector.tensor_tensor(
+                w_packed[:],
+                probs[g][:].rearrange("p t q -> p q t"),
+                vs_turned[:, :, VS_ROW].unsqueeze(1).to_broadcast([P, NQ, PACK]),
+                MULT,
+            )
+            w_mx.append(w_packed)
+        for g in range(PASSES):
+            turn_values(0, g)
+        w_mx = [quantise(w_mx[g], "w%d" % g) for g in range(PASSES)]
+        for g in range(PASSES):
+            gather_values(1, [g])
+            turn_values(1, g)
+
+        for h in range(HALVES):
+            y = psum.tile([NQ, P], F32, name="y%d" % h)
+            for g in range(PASSES):
+                v_codes, v_bytes = quantise(v_packed[h][g], "v%d%d" % (h, g))
+                nc.tensor.matmul_mx(
+                    y[:],
+                    lhsT=w_mx[g][0][:].bitcast(FP8X4),
+                    lhsT_scale=w_mx[g][1][:],
+                    rhs=v_codes[:].bitcast(FP8X4),
+                    rhs_scale=v_bytes[:],
+                    start=(g == 0),
+                    stop=(g == PASSES - 1),
+                )
+            y_out = keep.tile([NQ, P], F32, name="y_out%d" % h)
+            nc.scalar.mul(y_out[:], y[:], 1.0 / 16.0)
+            nc.sync.dma_start(out[0, :, h * P : (h + 1) * P], y_out[:])

@@ -20,8 +20,7 @@ PASSES = SLOTS // (P * PACK)
 RUN = 8
 BLOCKS = SLOTS // (PACK * RUN)
 HALVES = DV // P
-KB_ROW = 4
-VS_ROW = 8
+ROW = P - 1
 
 FLOPS = 2 * NQ * SLOTS * (D + DV)
 BYTES = TOKENS * (D + D // 32 + 4 * DV + 8) + 4 * NQ * (D + DV) + 2 * SLOTS
@@ -46,47 +45,32 @@ def tile_attend_sigmoid_topk_kernel(tc, qT, k_words, k_scales, vT, vs, kb, offs,
         offsets = keep.tile([P, SLOTS // 16], U16, name="offsets")
         nc.sync.dma_start(offsets[:], offs)
 
-        q_raw = keep.tile([P, PACK, NQ], F32, name="q_raw")
+        kb_pool = keep.tile([P, TOKENS], F32, name="kb_pool")
+        nc.scalar.dma_start(kb_pool[ROW:, :], kb[0:1, :])
+        vs_pool = keep.tile([P, TOKENS], F32, name="vs_pool", tag="vs_then_values")
+        nc.scalar.dma_start(vs_pool[ROW:, :], vs[0:1, :])
+        q_raw = keep.tile([P, PACK, NQ], F32, name="q_raw", tag="q_raw_then_values", align_bytes=64)
         nc.sync.dma_start(q_raw[:], qT[0].rearrange("(p t) q -> p t q", t=PACK))
-        word_pool = keep.tile([P, TOKENS], U32, name="word_pool")
+        word_pool = keep.tile([P, TOKENS], U32, name="word_pool", tag="words_then_bytes")
         nc.sync.dma_start(word_pool[:].bitcast(I32), k_words[0].rearrange("p n t -> p (n t)").bitcast(I32))
 
-        v_pool0 = keep.tile([P, TOKENS], F32, name="v_pool0")
-        nc.sync.dma_start(v_pool0[:], vT[0:P, :])
-
-        byte_pool = keep.tile([P, TOKENS], U8, name="byte_pool", tag="bytes_then_kb")
+        byte_pool = keep.tile([P, TOKENS], U8, name="byte_pool", tag="bytes_then_vs")
         nc.vector.memset(byte_pool[:].bitcast(I32), 0)
         for quad in range(4):
-            nc.scalar.dma_start(
+            nc.sync.dma_start(
                 byte_pool[32 * quad : 32 * quad + 4, :].bitcast(I32),
                 k_scales[0, 4 * quad : 4 * quad + 4, :].bitcast(I32),
             )
-        kb_pool = keep.tile([P, TOKENS], F32, name="kb_pool", tag="kb_then_codes", align_bytes=64)
-        nc.vector.memset(kb_pool[:], 0.0)
-        nc.scalar.dma_start(kb_pool[KB_ROW : KB_ROW + 1, :], kb[0:1, :])
+        nc.vector.memset(kb_pool[:ROW, :], 0.0)
+
         ident_f32 = keep.tile([P, P], F32, name="ident_f32")
         make_identity(nc, ident_f32[:])
         ident_bf16 = keep.tile([P, P], BF16, name="ident_bf16")
         make_identity(nc, ident_bf16[:])
-
-        vs_pool = keep.tile([P, TOKENS], F32, name="vs_pool", tag="vs_then_values")
         for start in range(0, TOKENS, 1024):
-            nc.gpsimd.memset(vs_pool[:, start : start + 1024], 0.0)
-        nc.sync.dma_start(vs_pool[VS_ROW : VS_ROW + 1, :], vs[0:1, :])
+            nc.gpsimd.memset(vs_pool[:ROW, start : start + 1024], 0.0)
 
-        k_bytes_listed = keep.tile([P, SLOTS], U8, name="k_bytes_listed", tag="early1")
-        nc.vector.tensor_copy(k_bytes_listed[:], byte_pool[:].indirect(offsets[:]))
-        k_bytes = keep.tile([P, SLOTS], U8, name="k_bytes", align_bytes=64)
-        nc.vector.tensor_copy(
-            k_bytes[:].bitcast(I32).rearrange("p (t b w) -> p t b w", t=PACK, w=RUN // 4),
-            k_bytes_listed[:].bitcast(I32).rearrange("p (b t w) -> p t b w", t=PACK, w=RUN // 4),
-        )
-        kb_dealt = keep.tile([P, SLOTS], F32, name="kb_dealt", tag="bytes_then_kb")
-        nc.vector.tensor_copy(dealt(kb_dealt[:].bitcast(U32)), kb_pool[:].bitcast(U32).indirect(offsets[:]))
-        k_codes = keep.tile([P, SLOTS], U32, name="k_codes", tag="kb_then_codes", align_bytes=64)
-        nc.vector.tensor_copy(dealt(k_codes[:]), word_pool[:].indirect(offsets[:]))
-
-        q_packed = keep.tile([P, NQ, PACK], BF16, name="q_packed", align_bytes=64)
+        q_packed = keep.tile([P, NQ, PACK], BF16, name="q_packed", tag="q_packed_then_values", align_bytes=64)
         nc.scalar.copy(
             q_packed[:].rearrange("p (c i) t -> p c t i", i=4),
             q_raw[:].rearrange("p t (c i) -> p c t i", i=4),
@@ -95,11 +79,25 @@ def tile_attend_sigmoid_topk_kernel(tc, qT, k_words, k_scales, vT, vs, kb, offs,
         q_bytes = keep.tile([P, NQ], U8, name="q_bytes", align_bytes=64)
         nc.vector.quantize_mx(q_codes[:].bitcast(FP8X4), q_bytes[:], q_packed[:].rearrange("p q t -> p (q t)"))
 
-        v_pool1 = keep.tile([P, TOKENS], F32, name="v_pool1", tag="early1")
-        nc.sync.dma_start(v_pool1[:], vT[P : 2 * P, :])
-        v_pool = [v_pool0, v_pool1]
+        v_pool = [
+            keep.tile([P, TOKENS], F32, name="v_pool0", tag="q_raw_then_values", align_bytes=64),
+            keep.tile([P, TOKENS], F32, name="v_pool1", tag="q_packed_then_values", align_bytes=64),
+        ]
+        for h in range(HALVES):
+            nc.sync.dma_start(v_pool[h][:], vT[h * P : (h + 1) * P, :])
 
-        vs_dealt = keep.tile([P, SLOTS], F32, name="vs_dealt")
+        kb_dealt = keep.tile([P, SLOTS], F32, name="kb_dealt")
+        nc.vector.tensor_copy(dealt(kb_dealt[:].bitcast(U32)), kb_pool[:].bitcast(U32).indirect(offsets[:]))
+        k_codes = keep.tile([P, SLOTS], U32, name="k_codes", align_bytes=64)
+        nc.vector.tensor_copy(dealt(k_codes[:]), word_pool[:].indirect(offsets[:]))
+        k_bytes_listed = keep.tile([P, SLOTS], U8, name="k_bytes_listed", tag="words_then_bytes")
+        nc.vector.tensor_copy(k_bytes_listed[:], byte_pool[:].indirect(offsets[:]))
+        k_bytes = keep.tile([P, SLOTS], U8, name="k_bytes", align_bytes=64)
+        nc.vector.tensor_copy(
+            k_bytes[:].bitcast(I32).rearrange("p (t b w) -> p t b w", t=PACK, w=RUN // 4),
+            k_bytes_listed[:].bitcast(I32).rearrange("p (b t w) -> p t b w", t=PACK, w=RUN // 4),
+        )
+        vs_dealt = keep.tile([P, SLOTS], F32, name="vs_dealt", tag="bytes_then_vs")
         nc.vector.tensor_copy(dealt(vs_dealt[:].bitcast(U32)), vs_pool[:].bitcast(U32).indirect(offsets[:]))
 
         probs = []
@@ -108,7 +106,7 @@ def tile_attend_sigmoid_topk_kernel(tc, qT, k_words, k_scales, vT, vs, kb, offs,
             for t in range(PACK):
                 nc.tensor.transpose(kb_turned[:, t, :], kb_dealt[:, slot_tile(g, t)], ident_f32[:])
             kb_col = keep.tile([P, PACK], F32, name="kb_col%d" % g)
-            nc.scalar.copy(kb_col[:], kb_turned[:, :, KB_ROW])
+            nc.scalar.copy(kb_col[:], kb_turned[:, :, ROW])
             scores = psum.tile([P, PACK, NQ], F32, name="scores%d" % g)
             for t in range(PACK):
                 nc.tensor.matmul_mx(
@@ -130,61 +128,69 @@ def tile_attend_sigmoid_topk_kernel(tc, qT, k_words, k_scales, vT, vs, kb, offs,
             columns = slice(passes[0] * 32, (passes[-1] + 1) * 32)
             nc.vector.tensor_copy(dealt(v_dealt[h][:])[:, blocks], v_pool[h][:].indirect(offsets[:, columns]))
 
-        def turn_values(h, g):
+        def turn_values(h, g, packed):
             v_turned = turn.tile([P, PACK, P], BF16, name="v_turned", tag="turned")
             for t in range(PACK):
                 nc.tensor.transpose(v_turned[:, t, :], v_dealt[h][:, slot_tile(g, t)], ident_bf16[:])
-            nc.scalar.copy(v_packed[h][g][:], v_turned[:].rearrange("p t e -> p e t"))
-
-        def quantise(packed, name):
-            codes = keep.tile([P, P], U32, name=name + "_codes", align_bytes=64)
-            scale_bytes = keep.tile([P, P], U8, name=name + "_bytes", align_bytes=64)
-            nc.vector.quantize_mx(codes[:].bitcast(FP8X4), scale_bytes[:], packed[:].rearrange("p c t -> p (c t)"))
-            return codes, scale_bytes
+            nc.scalar.copy(packed, v_turned[:].rearrange("p t e -> p e t"))
 
         v_dealt = [
             keep.tile([P, SLOTS], BF16, name="v_dealt0", tag="vs_then_values"),
             keep.tile([P, SLOTS], BF16, name="v_dealt1"),
         ]
-        v_packed = [
-            [keep.tile([P, P, PACK], BF16, name="v_packed%d%d" % (h, g), align_bytes=64) for g in range(PASSES)]
-            for h in range(HALVES)
-        ]
 
         gather_values(0, [0, 1])
-        w_mx = []
+        early_packed = keep.tile(
+            [P, 2 * PASSES * P, PACK], BF16, name="early_packed", tag="q_raw_then_values", align_bytes=64
+        )
         for g in range(PASSES):
             vs_turned = psum.tile([P, PACK, P], F32, name="vs_turned%d" % g)
             for t in range(PACK):
                 nc.tensor.transpose(vs_turned[:, t, :], vs_dealt[:, slot_tile(g, t)], ident_f32[:])
-            w_packed = keep.tile([P, NQ, PACK], BF16, name="w_packed%d" % g, align_bytes=64)
             nc.vector.tensor_tensor(
-                w_packed[:],
+                early_packed[:, g * P : (g + 1) * P, :],
                 probs[g][:].rearrange("p t q -> p q t"),
-                vs_turned[:, :, VS_ROW].unsqueeze(1).to_broadcast([P, NQ, PACK]),
+                vs_turned[:, :, ROW].unsqueeze(1).to_broadcast([P, NQ, PACK]),
                 MULT,
             )
-            w_mx.append(w_packed)
         for g in range(PASSES):
-            turn_values(0, g)
-        w_mx = [quantise(w_mx[g], "w%d" % g) for g in range(PASSES)]
+            turn_values(0, g, early_packed[:, (PASSES + g) * P : (PASSES + g + 1) * P, :])
+        late_packed = [keep.tile([P, P, PACK], BF16, name="late_packed%d" % g, align_bytes=64) for g in range(PASSES)]
         for g in range(PASSES):
             gather_values(1, [g])
-            turn_values(1, g)
+            turn_values(1, g, late_packed[g][:])
+
+        early_codes = keep.tile(
+            [P, 2 * PASSES * P], U32, name="early_codes", tag="q_packed_then_values", align_bytes=64
+        )
+        early_bytes = keep.tile([P, 2 * PASSES * P], U8, name="early_bytes", align_bytes=64)
+        nc.vector.quantize_mx(
+            early_codes[:].bitcast(FP8X4), early_bytes[:], early_packed[:].rearrange("p c t -> p (c t)")
+        )
+        late_codes = [keep.tile([P, P], U32, name="late_codes%d" % g, align_bytes=64) for g in range(PASSES)]
+        late_bytes = [keep.tile([P, P], U8, name="late_bytes%d" % g, align_bytes=64) for g in range(PASSES)]
+        for g in range(PASSES):
+            nc.vector.quantize_mx(
+                late_codes[g][:].bitcast(FP8X4), late_bytes[g][:], late_packed[g][:].rearrange("p c t -> p (c t)")
+            )
 
         for h in range(HALVES):
             y = psum.tile([NQ, P], F32, name="y%d" % h)
             for g in range(PASSES):
-                v_codes, v_bytes = quantise(v_packed[h][g], "v%d%d" % (h, g))
+                w_cols = slice(g * P, (g + 1) * P)
+                v_cols = slice((PASSES + g) * P, (PASSES + g + 1) * P)
                 nc.tensor.matmul_mx(
                     y[:],
-                    lhsT=w_mx[g][0][:].bitcast(FP8X4),
-                    lhsT_scale=w_mx[g][1][:],
-                    rhs=v_codes[:].bitcast(FP8X4),
-                    rhs_scale=v_bytes[:],
+                    lhsT=early_codes[:, w_cols].bitcast(FP8X4),
+                    lhsT_scale=early_bytes[:, w_cols],
+                    rhs=(early_codes[:, v_cols] if h == 0 else late_codes[g][:]).bitcast(FP8X4),
+                    rhs_scale=early_bytes[:, v_cols] if h == 0 else late_bytes[g][:],
                     start=(g == 0),
                     stop=(g == PASSES - 1),
                 )
             y_out = keep.tile([NQ, P], F32, name="y_out%d" % h)
-            nc.scalar.mul(y_out[:], y[:], 1.0 / 16.0)
+            if h == 0:
+                nc.scalar.mul(y_out[:], y[:], 1.0 / 16.0)
+            else:
+                nc.vector.tensor_scalar_mul(y_out[:], y[:], 1.0 / 16.0)
             nc.sync.dma_start(out[0, :, h * P : (h + 1) * P], y_out[:])

@@ -11,28 +11,21 @@ U16 = mybir.dt.uint16
 U8 = mybir.dt.uint8
 FP8X4 = mybir.dt.float8_e4m3fn_x4
 MULT = mybir.AluOpType.mult
+COPY = mybir.ActivationFunctionType.Copy
 SIGMOID = mybir.ActivationFunctionType.Sigmoid
 
 P = 128
 TOKENS, SLOTS, D, DV, NQ = 4096, 1024, 512, 256, 128
 PACK = 4
-PASSES = SLOTS // (P * PACK)
-RUN = 8
-BLOCKS = SLOTS // (PACK * RUN)
-HALVES = DV // P
+PASS_SLOTS = P * PACK
+PASSES = SLOTS // PASS_SLOTS
+LIST_COLUMNS = PASS_SLOTS // 16
 ROW = P - 1
+CAST_CHUNKS = 4
+CHUNK = TOKENS // CAST_CHUNKS
 
 FLOPS = 2 * NQ * SLOTS * (D + DV)
 BYTES = TOKENS * (D + D // 32 + 4 * DV + 8) + 4 * NQ * (D + DV) + 2 * SLOTS
-
-
-def dealt(ap):
-    return ap.rearrange("p (t b j) -> p b t j", t=PACK, j=RUN)
-
-
-def slot_tile(g, t):
-    start = (t * PASSES + g) * P
-    return slice(start, start + P)
 
 
 def tile_attend_sigmoid_topk_kernel(tc, qT, k_words, k_scales, vT, vs, kb, offs, out):
@@ -44,75 +37,114 @@ def tile_attend_sigmoid_topk_kernel(tc, qT, k_words, k_scales, vT, vs, kb, offs,
 
         offsets = keep.tile([P, SLOTS // 16], U16, name="offsets")
         nc.sync.dma_start(offsets[:], offs)
+        pass_offsets = [offsets[:, g * LIST_COLUMNS : (g + 1) * LIST_COLUMNS] for g in range(PASSES)]
 
         kb_pool = keep.tile([P, TOKENS], F32, name="kb_pool")
         nc.scalar.dma_start(kb_pool[ROW:, :], kb[0:1, :])
-        vs_pool = keep.tile([P, TOKENS], F32, name="vs_pool", tag="vs_then_values")
+        vs_pool = keep.tile([P, TOKENS], F32, name="vs_pool")
         nc.scalar.dma_start(vs_pool[ROW:, :], vs[0:1, :])
-        q_raw = keep.tile([P, PACK, NQ], F32, name="q_raw", tag="q_raw_then_values", align_bytes=64)
+        q_raw = keep.tile([P, PACK, NQ], F32, name="q_raw", tag="q_raw_then_words")
         nc.sync.dma_start(q_raw[:], qT[0].rearrange("(p t) q -> p t q", t=PACK))
-        word_pool = keep.tile([P, TOKENS], U32, name="word_pool", tag="words_then_bytes")
-        nc.sync.dma_start(word_pool[:].bitcast(I32), k_words[0].rearrange("p n t -> p (n t)").bitcast(I32))
+        v_low_chunks = [keep.tile([P, CHUNK], F32, name="v_low_chunk%d" % c, tag="chunk%d" % c, align_bytes=64) for c in range(CAST_CHUNKS)]
+        for c in range(CAST_CHUNKS):
+            nc.sync.dma_start(v_low_chunks[c][:], vT[0:P, c * CHUNK : (c + 1) * CHUNK])
 
-        byte_pool = keep.tile([P, TOKENS], U8, name="byte_pool", tag="bytes_then_vs")
+        byte_pool = keep.tile([P, TOKENS], U8, name="byte_pool")
         nc.vector.memset(byte_pool[:].bitcast(I32), 0)
         for quad in range(4):
             nc.sync.dma_start(
                 byte_pool[32 * quad : 32 * quad + 4, :].bitcast(I32),
                 k_scales[0, 4 * quad : 4 * quad + 4, :].bitcast(I32),
             )
-        nc.vector.memset(kb_pool[:ROW, :], 0.0)
+        nc.vector.memset(kb_pool[:ROW, :].bitcast(I32), 0)
+        nc.vector.memset(vs_pool[:ROW, :].bitcast(I32), 0)
 
-        ident_f32 = keep.tile([P, P], F32, name="ident_f32")
-        make_identity(nc, ident_f32[:])
-        ident_bf16 = keep.tile([P, P], BF16, name="ident_bf16")
-        make_identity(nc, ident_bf16[:])
-        for start in range(0, TOKENS, 1024):
-            nc.gpsimd.memset(vs_pool[:ROW, start : start + 1024], 0.0)
+        identity = keep.tile([P, P], F32, name="identity")
+        make_identity(nc, identity[:])
 
-        q_packed = keep.tile([P, NQ, PACK], BF16, name="q_packed", tag="q_packed_then_values", align_bytes=64)
+        def quantise(packed, name):
+            codes = keep.tile([P, packed.shape[1]], U32, name=name + "_codes", align_bytes=64)
+            scale_bytes = keep.tile([P, packed.shape[1]], U8, name=name + "_bytes", align_bytes=64)
+            nc.vector.quantize_mx(codes[:].bitcast(FP8X4), scale_bytes[:], packed.rearrange("p c t -> p (c t)"))
+            return codes, scale_bytes
+
+        q_packed = keep.tile([P, NQ, PACK], BF16, name="q_packed", align_bytes=64)
         nc.scalar.copy(
             q_packed[:].rearrange("p (c i) t -> p c t i", i=4),
             q_raw[:].rearrange("p t (c i) -> p c t i", i=4),
         )
-        q_codes = keep.tile([P, NQ], U32, name="q_codes", align_bytes=64)
-        q_bytes = keep.tile([P, NQ], U8, name="q_bytes", align_bytes=64)
-        nc.vector.quantize_mx(q_codes[:].bitcast(FP8X4), q_bytes[:], q_packed[:].rearrange("p q t -> p (q t)"))
+        q_codes, q_bytes = quantise(q_packed[:], "q")
 
-        v_pool = [
-            keep.tile([P, TOKENS], F32, name="v_pool0", tag="q_raw_then_values", align_bytes=64),
-            keep.tile([P, TOKENS], F32, name="v_pool1", tag="q_packed_then_values", align_bytes=64),
-        ]
-        for h in range(HALVES):
-            nc.sync.dma_start(v_pool[h][:], vT[h * P : (h + 1) * P, :])
+        word_pool = keep.tile([P, TOKENS], U32, name="word_pool", tag="q_raw_then_words")
+        nc.sync.dma_start(word_pool[:].bitcast(I32), k_words[0].rearrange("p n t -> p (n t)").bitcast(I32))
 
-        kb_dealt = keep.tile([P, SLOTS], F32, name="kb_dealt")
-        nc.vector.tensor_copy(dealt(kb_dealt[:].bitcast(U32)), kb_pool[:].bitcast(U32).indirect(offsets[:]))
-        k_codes = keep.tile([P, SLOTS], U32, name="k_codes", align_bytes=64)
-        nc.vector.tensor_copy(dealt(k_codes[:]), word_pool[:].indirect(offsets[:]))
-        k_bytes_listed = keep.tile([P, SLOTS], U8, name="k_bytes_listed", tag="words_then_bytes")
+        v_low_pool = keep.tile([P, TOKENS], BF16, name="v_low_pool")
+        for c in range(CAST_CHUNKS):
+            nc.scalar.activation(v_low_pool[:, c * CHUNK : (c + 1) * CHUNK], v_low_chunks[c][:], COPY)
+        v_high_pool = keep.tile([P, TOKENS], F32, name="v_high_pool", tag="chunk1", align_bytes=64)
+        nc.sync.dma_start(v_high_pool[:], vT[P : 2 * P, :])
+        v_low_listed = keep.tile([P, SLOTS], BF16, name="v_low_listed")
+        nc.scalar.activation(v_low_listed[:], v_low_pool[:].indirect(offsets[:]), COPY)
+
+        kb_listed = keep.tile([P, SLOTS], F32, name="kb_listed")
+        nc.vector.tensor_copy(kb_listed[:], kb_pool[:].indirect(offsets[:]))
+        vs_listed = keep.tile([P, SLOTS], F32, name="vs_listed")
+        nc.vector.tensor_copy(vs_listed[:], vs_pool[:].indirect(offsets[:]))
+        k_bytes_listed = keep.tile([P, SLOTS], U8, name="k_bytes_listed")
         nc.vector.tensor_copy(k_bytes_listed[:], byte_pool[:].indirect(offsets[:]))
-        k_bytes = keep.tile([P, SLOTS], U8, name="k_bytes", align_bytes=64)
+        k_bytes = keep.tile([P, PACK, PASSES * P], U8, name="k_bytes", align_bytes=64)
         nc.vector.tensor_copy(
-            k_bytes[:].bitcast(I32).rearrange("p (t b w) -> p t b w", t=PACK, w=RUN // 4),
-            k_bytes_listed[:].bitcast(I32).rearrange("p (b t w) -> p t b w", t=PACK, w=RUN // 4),
+            k_bytes[:].rearrange("p t (c i) -> p c t i", i=16),
+            k_bytes_listed[:].rearrange("p (c i t) -> p c t i", i=16, t=PACK),
         )
-        vs_dealt = keep.tile([P, SLOTS], F32, name="vs_dealt", tag="bytes_then_vs")
-        nc.vector.tensor_copy(dealt(vs_dealt[:].bitcast(U32)), vs_pool[:].bitcast(U32).indirect(offsets[:]))
+
+        def turn_row(listed, g, turned):
+            for t in range(PACK):
+                nc.tensor.transpose(
+                    turned[:, t, :], listed[:, g * PASS_SLOTS + t : (g + 1) * PASS_SLOTS : PACK], identity[:]
+                )
+
+        def turn_values(listed, packed):
+            words = listed[:].bitcast(F32)
+            passes = words.shape[1] // (2 * P)
+            v_turned = turn.tile([P, passes, 2, P], F32, name="v_turned", tag="turned")
+            for g in range(passes):
+                for u in range(2):
+                    nc.tensor.transpose(v_turned[:, g, u, :], words[:, 2 * P * g + u : 2 * P * (g + 1) : 2], identity[:])
+            nc.scalar.copy(
+                packed.rearrange("p c t -> p (c t)").bitcast(F32).rearrange("p (g e u) -> p g e u", g=passes, u=2),
+                v_turned[:].rearrange("p g u e -> p g e u"),
+            )
+
+        kb_columns = keep.tile([P, PASSES, PACK], F32, name="kb_columns", tag="chunk%d" % (CAST_CHUNKS - 1), align_bytes=64)
+        vs_turned = []
+        for g in range(PASSES):
+            kb_turned = turn.tile([P, PACK, P], F32, name="kb_turned", tag="turned")
+            turn_row(kb_listed, g, kb_turned)
+            nc.scalar.copy(kb_columns[:, g, :], kb_turned[:, :, ROW])
+        for g in range(PASSES):
+            vs_turned.append(psum.tile([P, PACK, P], F32, name="vs_turned%d" % g))
+            turn_row(vs_listed, g, vs_turned[g])
+
+        v_low_packed = keep.tile([P, PASSES * P, PACK], BF16, name="v_low_packed", align_bytes=64)
+        turn_values(v_low_listed, v_low_packed[:])
+        v_low_codes, v_low_bytes = quantise(v_low_packed[:], "v_low")
 
         probs = []
         for g in range(PASSES):
-            kb_turned = turn.tile([P, PACK, P], F32, name="kb_turned", tag="turned")
-            for t in range(PACK):
-                nc.tensor.transpose(kb_turned[:, t, :], kb_dealt[:, slot_tile(g, t)], ident_f32[:])
-            kb_col = keep.tile([P, PACK], F32, name="kb_col%d" % g)
-            nc.scalar.copy(kb_col[:], kb_turned[:, :, ROW])
+            k_codes_listed = keep.tile([P, PASS_SLOTS], U32, name="k_codes_listed", tag="k_codes_listed")
+            nc.vector.tensor_copy(k_codes_listed[:], word_pool[:].indirect(pass_offsets[g]))
+            k_codes = keep.tile([P, PACK, P], U32, name="k_codes%d" % g, align_bytes=64)
+            nc.vector.tensor_copy(
+                k_codes[:].bitcast(I32).rearrange("p t (c i) -> p c t i", i=4),
+                k_codes_listed[:].bitcast(I32).rearrange("p (c i t) -> p c t i", i=4, t=PACK),
+            )
             scores = psum.tile([P, PACK, NQ], F32, name="scores%d" % g)
             for t in range(PACK):
                 nc.tensor.matmul_mx(
                     scores[:, t, :],
-                    lhsT=k_codes[:, slot_tile(g, t)].bitcast(FP8X4),
-                    lhsT_scale=k_bytes[:, slot_tile(g, t)],
+                    lhsT=k_codes[:, t, :].bitcast(FP8X4),
+                    lhsT_scale=k_bytes[:, t, g * P : (g + 1) * P],
                     rhs=q_codes[:].bitcast(FP8X4),
                     rhs_scale=q_bytes[:],
                     start=True,
@@ -120,77 +152,40 @@ def tile_attend_sigmoid_topk_kernel(tc, qT, k_words, k_scales, vT, vs, kb, offs,
                 )
             prob = keep.tile([P, PACK, NQ], F32, name="prob%d" % g)
             for t in range(PACK):
-                nc.scalar.activation(prob[:, t, :], scores[:, t, :], SIGMOID, bias=kb_col[:, t : t + 1])
+                nc.scalar.activation(prob[:, t, :], scores[:, t, :], SIGMOID, bias=kb_columns[:, g, t : t + 1])
             probs.append(prob)
 
-        def gather_values(h, passes):
-            blocks = slice(passes[0] * BLOCKS // PASSES, (passes[-1] + 1) * BLOCKS // PASSES)
-            columns = slice(passes[0] * 32, (passes[-1] + 1) * 32)
-            nc.vector.tensor_copy(dealt(v_dealt[h][:])[:, blocks], v_pool[h][:].indirect(offsets[:, columns]))
-
-        def turn_values(h, g, packed):
-            v_turned = turn.tile([P, PACK, P], BF16, name="v_turned", tag="turned")
-            for t in range(PACK):
-                nc.tensor.transpose(v_turned[:, t, :], v_dealt[h][:, slot_tile(g, t)], ident_bf16[:])
-            nc.scalar.copy(packed, v_turned[:].rearrange("p t e -> p e t"))
-
-        v_dealt = [
-            keep.tile([P, SLOTS], BF16, name="v_dealt0", tag="vs_then_values"),
-            keep.tile([P, SLOTS], BF16, name="v_dealt1"),
-        ]
-
-        gather_values(0, [0, 1])
-        early_packed = keep.tile(
-            [P, 2 * PASSES * P, PACK], BF16, name="early_packed", tag="q_raw_then_values", align_bytes=64
-        )
+        v_high_packed = keep.tile([P, PASSES * P, PACK], BF16, name="v_high_packed", align_bytes=64)
         for g in range(PASSES):
-            vs_turned = psum.tile([P, PACK, P], F32, name="vs_turned%d" % g)
-            for t in range(PACK):
-                nc.tensor.transpose(vs_turned[:, t, :], vs_dealt[:, slot_tile(g, t)], ident_f32[:])
+            v_high_listed = keep.tile([P, PASS_SLOTS], BF16, name="v_high_listed%d" % g)
+            nc.vector.tensor_copy(v_high_listed[:], v_high_pool[:].indirect(pass_offsets[g]))
+            turn_values(v_high_listed, v_high_packed[:, g * P : (g + 1) * P, :])
+
+        w_packed = keep.tile([P, PASSES * NQ, PACK], BF16, name="w_packed", tag="chunk1", align_bytes=64)
+        for g in range(PASSES):
             nc.vector.tensor_tensor(
-                early_packed[:, g * P : (g + 1) * P, :],
+                w_packed[:, g * NQ : (g + 1) * NQ, :],
                 probs[g][:].rearrange("p t q -> p q t"),
-                vs_turned[:, :, ROW].unsqueeze(1).to_broadcast([P, NQ, PACK]),
+                vs_turned[g][:, :, ROW].unsqueeze(1).to_broadcast([P, NQ, PACK]),
                 MULT,
             )
-        for g in range(PASSES):
-            turn_values(0, g, early_packed[:, (PASSES + g) * P : (PASSES + g + 1) * P, :])
-        late_packed = [keep.tile([P, P, PACK], BF16, name="late_packed%d" % g, align_bytes=64) for g in range(PASSES)]
-        for g in range(PASSES):
-            gather_values(1, [g])
-            turn_values(1, g, late_packed[g][:])
+        w_mx = [quantise(w_packed[:, 0:NQ, :], "w0")]
+        v_mx = [(v_low_codes, v_low_bytes), quantise(v_high_packed[:], "v_high")]
+        w_mx.append(quantise(w_packed[:, NQ : 2 * NQ, :], "w1"))
 
-        early_codes = keep.tile(
-            [P, 2 * PASSES * P], U32, name="early_codes", tag="q_packed_then_values", align_bytes=64
-        )
-        early_bytes = keep.tile([P, 2 * PASSES * P], U8, name="early_bytes", align_bytes=64)
-        nc.vector.quantize_mx(
-            early_codes[:].bitcast(FP8X4), early_bytes[:], early_packed[:].rearrange("p c t -> p (c t)")
-        )
-        late_codes = [keep.tile([P, P], U32, name="late_codes%d" % g, align_bytes=64) for g in range(PASSES)]
-        late_bytes = [keep.tile([P, P], U8, name="late_bytes%d" % g, align_bytes=64) for g in range(PASSES)]
+        y = [psum.tile([NQ, P], F32, name="y%d" % h) for h in range(2)]
         for g in range(PASSES):
-            nc.vector.quantize_mx(
-                late_codes[g][:].bitcast(FP8X4), late_bytes[g][:], late_packed[g][:].rearrange("p c t -> p (c t)")
-            )
-
-        for h in range(HALVES):
-            y = psum.tile([NQ, P], F32, name="y%d" % h)
-            for g in range(PASSES):
-                w_cols = slice(g * P, (g + 1) * P)
-                v_cols = slice((PASSES + g) * P, (PASSES + g + 1) * P)
+            for h in range(2):
                 nc.tensor.matmul_mx(
-                    y[:],
-                    lhsT=early_codes[:, w_cols].bitcast(FP8X4),
-                    lhsT_scale=early_bytes[:, w_cols],
-                    rhs=(early_codes[:, v_cols] if h == 0 else late_codes[g][:]).bitcast(FP8X4),
-                    rhs_scale=early_bytes[:, v_cols] if h == 0 else late_bytes[g][:],
+                    y[h][:],
+                    lhsT=w_mx[g][0][:].bitcast(FP8X4),
+                    lhsT_scale=w_mx[g][1][:],
+                    rhs=v_mx[h][0][:, g * P : (g + 1) * P].bitcast(FP8X4),
+                    rhs_scale=v_mx[h][1][:, g * P : (g + 1) * P],
                     start=(g == 0),
                     stop=(g == PASSES - 1),
                 )
-            y_out = keep.tile([NQ, P], F32, name="y_out%d" % h)
-            if h == 0:
-                nc.scalar.mul(y_out[:], y[:], 1.0 / 16.0)
-            else:
-                nc.vector.tensor_scalar_mul(y_out[:], y[:], 1.0 / 16.0)
-            nc.sync.dma_start(out[0, :, h * P : (h + 1) * P], y_out[:])
+        y_out = keep.tile([NQ, DV], F32, name="y_out")
+        nc.scalar.mul(y_out[:, 0:P], y[0][:], 1.0 / 16.0)
+        nc.vector.tensor_scalar_mul(y_out[:, P:DV], y[1][:], 1.0 / 16.0)
+        nc.sync.dma_start(out[0], y_out[:])

@@ -51,11 +51,8 @@ def tile_attend_sigmoid_topk_kernel(tc, qT, k_words, k_scales, vT, vs, kb, offs,
 
         byte_pool = keep.tile([P, TOKENS], U8, name="byte_pool")
         nc.vector.memset(byte_pool[:].bitcast(I32), 0)
-        for quad in range(4):
-            nc.sync.dma_start(
-                byte_pool[32 * quad : 32 * quad + 4, :].bitcast(I32),
-                k_scales[0, 4 * quad : 4 * quad + 4, :].bitcast(I32),
-            )
+        for r in range(4):
+            nc.sync.dma_start(byte_pool[r:P:32, :].bitcast(I32), k_scales[0, r:16:4, :].bitcast(I32))
         nc.vector.memset(kb_pool[:ROW, :].bitcast(I32), 0)
         nc.vector.memset(vs_pool[:ROW, :].bitcast(I32), 0)
 

from contextlib import ExitStack

import concourse.mybir as mybir
from concourse.masks import make_identity

F32 = mybir.dt.float32
BF16 = mybir.dt.bfloat16
I32 = mybir.dt.int32
U32 = mybir.dt.uint32
U16 = mybir.dt.uint16
U8 = mybir.dt.uint8
FP8X4 = mybir.dt.float8_e4m3fn_x4
MULT = mybir.AluOpType.mult
COPY = mybir.ActivationFunctionType.Copy
SIGMOID = mybir.ActivationFunctionType.Sigmoid

P = 128
TOKENS, SLOTS, D, DV, NQ = 4096, 1024, 512, 256, 128
PACK = 4
PASS_SLOTS = P * PACK
PASSES = SLOTS // PASS_SLOTS
LIST_COLUMNS = PASS_SLOTS // 16
ROW = P - 1
CAST_CHUNKS = 4
CHUNK = TOKENS // CAST_CHUNKS

FLOPS = 2 * NQ * SLOTS * (D + DV)
BYTES = TOKENS * (D + D // 32 + 4 * DV + 8) + 4 * NQ * (D + DV) + 2 * SLOTS


def tile_attend_sigmoid_topk_kernel(tc, qT, k_words, k_scales, vT, vs, kb, offs, out):
    nc = tc.nc
    with ExitStack() as ctx:
        keep = ctx.enter_context(tc.tile_pool(name="keep", bufs=1))
        psum = ctx.enter_context(tc.psum_pool(name="psum", bufs=1))
        turn = ctx.enter_context(tc.psum_pool(name="turn", bufs=2))

        offsets = keep.tile([P, SLOTS // 16], U16, name="offsets")
        nc.sync.dma_start(offsets[:], offs)
        pass_offsets = [offsets[:, g * LIST_COLUMNS : (g + 1) * LIST_COLUMNS] for g in range(PASSES)]

        kb_pool = keep.tile([P, TOKENS], F32, name="kb_pool")
        nc.scalar.dma_start(kb_pool[ROW:, :], kb[0:1, :])
        vs_pool = keep.tile([P, TOKENS], F32, name="vs_pool")
        nc.scalar.dma_start(vs_pool[ROW:, :], vs[0:1, :])
        q_raw = keep.tile([P, PACK, NQ], F32, name="q_raw", tag="q_raw_then_words")
        nc.sync.dma_start(q_raw[:], qT[0].rearrange("(p t) q -> p t q", t=PACK))
        v_low_chunks = [keep.tile([P, CHUNK], F32, name="v_low_chunk%d" % c, tag="chunk%d" % c, align_bytes=64) for c in range(CAST_CHUNKS)]
        for c in range(CAST_CHUNKS):
            nc.sync.dma_start(v_low_chunks[c][:], vT[0:P, c * CHUNK : (c + 1) * CHUNK])

        byte_pool = keep.tile([P, TOKENS], U8, name="byte_pool")
        nc.vector.memset(byte_pool[:].bitcast(I32), 0)
        for r in range(4):
            nc.sync.dma_start(byte_pool[r:P:32, :].bitcast(I32), k_scales[0, r:16:4, :].bitcast(I32))
        nc.vector.memset(kb_pool[:ROW, :].bitcast(I32), 0)
        nc.vector.memset(vs_pool[:ROW, :].bitcast(I32), 0)

        identity = keep.tile([P, P], F32, name="identity")
        make_identity(nc, identity[:])

        def quantise(packed, name):
            codes = keep.tile([P, packed.shape[1]], U32, name=name + "_codes", align_bytes=64)
            scale_bytes = keep.tile([P, packed.shape[1]], U8, name=name + "_bytes", align_bytes=64)
            nc.vector.quantize_mx(codes[:].bitcast(FP8X4), scale_bytes[:], packed.rearrange("p c t -> p (c t)"))
            return codes, scale_bytes

        q_packed = keep.tile([P, NQ, PACK], BF16, name="q_packed", align_bytes=64)
        nc.scalar.copy(
            q_packed[:].rearrange("p (c i) t -> p c t i", i=4),
            q_raw[:].rearrange("p t (c i) -> p c t i", i=4),
        )
        q_codes, q_bytes = quantise(q_packed[:], "q")

        word_pool = keep.tile([P, TOKENS], U32, name="word_pool", tag="q_raw_then_words")
        nc.sync.dma_start(word_pool[:].bitcast(I32), k_words[0].rearrange("p n t -> p (n t)").bitcast(I32))

        v_low_pool = keep.tile([P, TOKENS], BF16, name="v_low_pool")
        for c in range(CAST_CHUNKS):
            nc.scalar.activation(v_low_pool[:, c * CHUNK : (c + 1) * CHUNK], v_low_chunks[c][:], COPY)
        v_high_pool = keep.tile([P, TOKENS], F32, name="v_high_pool", tag="chunk1", align_bytes=64)
        nc.sync.dma_start(v_high_pool[:], vT[P : 2 * P, :])
        v_low_listed = keep.tile([P, SLOTS], BF16, name="v_low_listed")
        nc.scalar.activation(v_low_listed[:], v_low_pool[:].indirect(offsets[:]), COPY)

        kb_listed = keep.tile([P, SLOTS], F32, name="kb_listed")
        nc.vector.tensor_copy(kb_listed[:], kb_pool[:].indirect(offsets[:]))
        vs_listed = keep.tile([P, SLOTS], F32, name="vs_listed")
        nc.vector.tensor_copy(vs_listed[:], vs_pool[:].indirect(offsets[:]))
        k_bytes_listed = keep.tile([P, SLOTS], U8, name="k_bytes_listed")
        nc.vector.tensor_copy(k_bytes_listed[:], byte_pool[:].indirect(offsets[:]))
        k_bytes = keep.tile([P, PACK, PASSES * P], U8, name="k_bytes", align_bytes=64)
        nc.vector.tensor_copy(
            k_bytes[:].rearrange("p t (c i) -> p c t i", i=16),
            k_bytes_listed[:].rearrange("p (c i t) -> p c t i", i=16, t=PACK),
        )

        def turn_row(listed, g, turned):
            for t in range(PACK):
                nc.tensor.transpose(
                    turned[:, t, :], listed[:, g * PASS_SLOTS + t : (g + 1) * PASS_SLOTS : PACK], identity[:]
                )

        def turn_values(listed, packed):
            words = listed[:].bitcast(F32)
            passes = words.shape[1] // (2 * P)
            v_turned = turn.tile([P, passes, 2, P], F32, name="v_turned", tag="turned")
            for g in range(passes):
                for u in range(2):
                    nc.tensor.transpose(v_turned[:, g, u, :], words[:, 2 * P * g + u : 2 * P * (g + 1) : 2], identity[:])
            nc.scalar.copy(
                packed.rearrange("p c t -> p (c t)").bitcast(F32).rearrange("p (g e u) -> p g e u", g=passes, u=2),
                v_turned[:].rearrange("p g u e -> p g e u"),
            )

        kb_columns = keep.tile([P, PASSES, PACK], F32, name="kb_columns", tag="chunk%d" % (CAST_CHUNKS - 1), align_bytes=64)
        vs_turned = []
        for g in range(PASSES):
            kb_turned = turn.tile([P, PACK, P], F32, name="kb_turned", tag="turned")
            turn_row(kb_listed, g, kb_turned)
            nc.scalar.copy(kb_columns[:, g, :], kb_turned[:, :, ROW])
        for g in range(PASSES):
            vs_turned.append(psum.tile([P, PACK, P], F32, name="vs_turned%d" % g))
            turn_row(vs_listed, g, vs_turned[g])

        v_low_packed = keep.tile([P, PASSES * P, PACK], BF16, name="v_low_packed", align_bytes=64)
        turn_values(v_low_listed, v_low_packed[:])
        v_low_codes, v_low_bytes = quantise(v_low_packed[:], "v_low")

        probs = []
        for g in range(PASSES):
            k_codes_listed = keep.tile([P, PASS_SLOTS], U32, name="k_codes_listed", tag="k_codes_listed")
            nc.vector.tensor_copy(k_codes_listed[:], word_pool[:].indirect(pass_offsets[g]))
            k_codes = keep.tile([P, PACK, P], U32, name="k_codes%d" % g, align_bytes=64)
            nc.vector.tensor_copy(
                k_codes[:].bitcast(I32).rearrange("p t (c i) -> p c t i", i=4),
                k_codes_listed[:].bitcast(I32).rearrange("p (c i t) -> p c t i", i=4, t=PACK),
            )
            scores = psum.tile([P, PACK, NQ], F32, name="scores%d" % g)
            for t in range(PACK):
                nc.tensor.matmul_mx(
                    scores[:, t, :],
                    lhsT=k_codes[:, t, :].bitcast(FP8X4),
                    lhsT_scale=k_bytes[:, t, g * P : (g + 1) * P],
                    rhs=q_codes[:].bitcast(FP8X4),
                    rhs_scale=q_bytes[:],
                    start=True,
                    stop=True,
                )
            prob = keep.tile([P, PACK, NQ], F32, name="prob%d" % g)
            for t in range(PACK):
                nc.scalar.activation(prob[:, t, :], scores[:, t, :], SIGMOID, bias=kb_columns[:, g, t : t + 1])
            probs.append(prob)

        v_high_packed = keep.tile([P, PASSES * P, PACK], BF16, name="v_high_packed", align_bytes=64)
        for g in range(PASSES):
            v_high_listed = keep.tile([P, PASS_SLOTS], BF16, name="v_high_listed%d" % g)
            nc.vector.tensor_copy(v_high_listed[:], v_high_pool[:].indirect(pass_offsets[g]))
            turn_values(v_high_listed, v_high_packed[:, g * P : (g + 1) * P, :])

        w_packed = keep.tile([P, PASSES * NQ, PACK], BF16, name="w_packed", tag="chunk1", align_bytes=64)
        for g in range(PASSES):
            nc.vector.tensor_tensor(
                w_packed[:, g * NQ : (g + 1) * NQ, :],
                probs[g][:].rearrange("p t q -> p q t"),
                vs_turned[g][:, :, ROW].unsqueeze(1).to_broadcast([P, NQ, PACK]),
                MULT,
            )
        w_mx = [quantise(w_packed[:, 0:NQ, :], "w0")]
        v_mx = [(v_low_codes, v_low_bytes), quantise(v_high_packed[:], "v_high")]
        w_mx.append(quantise(w_packed[:, NQ : 2 * NQ, :], "w1"))

        y = [psum.tile([NQ, P], F32, name="y%d" % h) for h in range(2)]
        for g in range(PASSES):
            for h in range(2):
                nc.tensor.matmul_mx(
                    y[h][:],
                    lhsT=w_mx[g][0][:].bitcast(FP8X4),
                    lhsT_scale=w_mx[g][1][:],
                    rhs=v_mx[h][0][:, g * P : (g + 1) * P].bitcast(FP8X4),
                    rhs_scale=v_mx[h][1][:, g * P : (g + 1) * P],
                    start=(g == 0),
                    stop=(g == PASSES - 1),
                )
        y_out = keep.tile([NQ, DV], F32, name="y_out")
        nc.scalar.mul(y_out[:, 0:P], y[0][:], 1.0 / 16.0)
        nc.vector.tensor_scalar_mul(y_out[:, P:DV], y[1][:], 1.0 / 16.0)
        nc.sync.dma_start(out[0], y_out[:])
